import numpy as np
import ml_dtypes


def mxq(x, axis, fmt="e4m3"):
    dtype, down = {"e4m3": (ml_dtypes.float8_e4m3fn, 7), "e5m2": (ml_dtypes.float8_e5m2, 14)}[fmt]
    v = np.moveaxis(np.asarray(x, np.float32).astype(ml_dtypes.bfloat16).astype(np.float64), axis, -1)
    blocks = v.reshape(v.shape[:-1] + (-1, 32))
    amax = np.abs(blocks).max(-1, keepdims=True)
    byte = np.maximum(np.where(amax > 0, np.frexp(amax)[1] - 1 + 127, 0) - down, 1)
    scale = np.exp2(byte - 127.0)
    codes = (blocks / scale).astype(np.float32).astype(dtype).astype(np.float64)
    return np.moveaxis((codes * scale).reshape(v.shape), -1, axis)


WIDE = False


def mx_kscale(k):
    if not WIDE:
        return np.ones(k)
    levels = np.array([10, -10, 5, -5, 0])
    if k % 512:
        return np.exp2(np.random.permutation(np.resize(levels, k // 32))).repeat(32)
    a = np.empty((k // 512, 16))
    for p in range(k // 512):
        a[p, :8] = np.random.permutation(np.resize(levels, 8))
        for g in range(8):
            far = levels[np.abs(levels - a[p, g]) >= 10]
            a[p, g + 8] = far[np.random.randint(len(far))]
    return np.exp2(a.ravel()).repeat(32)


def f64(x):
    return np.asarray(x).astype(np.float64)


def striped(idx):
    return np.tile(np.asarray(idx).reshape(-1, 16).T, (8, 1)).astype(np.uint16)


def unstriped(offs):
    return offs[:16].T.reshape(-1).astype(np.int64)


E2M1 = np.array([0.0, 0.5, 1.0, 1.5, 2.0, 3.0, 4.0, 6.0, -0.0, -0.5, -1.0, -1.5, -2.0, -3.0, -4.0, -6.0])


def pack_weight(w, fmt):
    k, n = w.shape
    w = f64(np.asarray(w, np.float32).astype(ml_dtypes.bfloat16)).reshape(k // 32, 32, n)
    amax = np.abs(w).max(1)
    if fmt == "e4m3":
        byte = np.frexp(amax)[1] - 1 + 127 - 7
    else:
        mant, ex = np.frexp(amax / 6.0)
        byte = np.where(mant > 0.5, ex, ex - 1) + 127
    byte = np.clip(np.where(amax > 0, byte, 1), 1, 254)
    scaled = (w * np.exp2(127.0 - byte)[:, None, :]).reshape(k, n).astype(np.float32)
    by_word = np.ascontiguousarray(scaled.reshape(k // 512, 128, 4, n).transpose(0, 1, 3, 2))
    if fmt == "e4m3":
        words = by_word.astype(ml_dtypes.float8_e4m3fn).view(np.uint8)
    else:
        c = by_word.astype(ml_dtypes.float4_e2m1fn).view(np.uint8) & 0xF
        words = (c[..., 0::2] | (c[..., 1::2] << 4)).reshape(k // 512, 128, 2 * n)
    return np.ascontiguousarray(words), np.ascontiguousarray(byte.astype(np.uint8).reshape(k // 512, 16, n))


def unpack_weight(words, scales, fmt):
    g, _, n = scales.shape
    words = np.ascontiguousarray(words).reshape(g, 128, n, -1)
    if fmt == "e4m3":
        vals = words.view(ml_dtypes.float8_e4m3fn).astype(np.float64)
    else:
        nib = np.empty((g, 128, n, 4), np.uint8)
        nib[..., 0::2] = words & 0xF
        nib[..., 1::2] = words >> 4
        vals = E2M1[nib]
    vals = vals * np.repeat(np.exp2(scales.astype(np.float64) - 127.0), 8, axis=1)[..., None]
    return vals.transpose(0, 1, 3, 2).reshape(g * 512, n)


K, L, M, T, J, N = 512, 512, 512, 512, 1024, 512


def setup_inputs():
    n = np.random.standard_normal
    idx = np.random.randint(0, T, J)
    idx2 = np.random.randint(0, T, J)
    idx3 = np.random.randint(0, T, J)
    fk = mx_kscale(K)
    fl = mx_kscale(L)
    fm = mx_kscale(M)
    bap = pack_weight(n((K, T)) / fk[:, None], "e2m1")
    wap = pack_weight(n((K, N)) * 1 / np.sqrt(K) * fk[:, None], "e4m3")
    wbp = pack_weight(n((L, N)) * 1 / np.sqrt(L) * fl[:, None], "e2m1")
    bcp = pack_weight(n((M, T)) / fm[:, None], "e2m1")
    wcp = pack_weight(n((M, N)) * 1 / np.sqrt(M) * fm[:, None], "e4m3")
    return {
        "ba_words": bap[0],
        "ba_scales": bap[1],
        "wa_words": wap[0],
        "wa_scales": wap[1],
        "bb": (n((L, T)) / fl[:, None]).astype(np.float32),
        "wb_words": wbp[0],
        "wb_scales": wbp[1],
        "bc_words": bcp[0],
        "bc_scales": bcp[1],
        "wc_words": wcp[0],
        "wc_scales": wcp[1],
        "sc1": (np.random.uniform(0.5, 2.0, (1, J))).astype(np.float32),
        "offs": striped(idx),
        "offs2": striped(idx2),
        "offs3": striped(idx3),
    }


def reference(ba_words, ba_scales, wa_words, wa_scales, bb, wb_words, wb_scales, bc_words, bc_scales, wc_words, wc_scales, sc1, offs, offs2, offs3):
    idx = unstriped(offs)
    idx2 = unstriped(offs2)
    idx3 = unstriped(offs3)
    bau = unpack_weight(ba_words, ba_scales, "e2m1")
    wau = unpack_weight(wa_words, wa_scales, "e4m3")
    wbu = unpack_weight(wb_words, wb_scales, "e2m1")
    bcu = unpack_weight(bc_words, bc_scales, "e2m1")
    wcu = unpack_weight(wc_words, wc_scales, "e4m3")
    za = wau.T @ bau
    bbq = mxq(f64(bb), 0, "e4m3")
    zb = wbu.T @ bbq
    zc = wcu.T @ bcu
    y = np.maximum(za[:, idx] + zb[:, idx2] + zc[:, idx3], 0.0) * f64(sc1)
    return y

@@ -1,0 +1,168 @@
+from contextlib import ExitStack
+
+import concourse.mybir as mybir
+from concourse.masks import make_identity
+
+K, T, J, N = 512, 512, 1024, 512
+FLOPS = 3 * 2 * K * T * N
+
+F32 = mybir.dt.float32
+BF16 = mybir.dt.bfloat16
+I32 = mybir.dt.int32
+U32 = mybir.dt.uint32
+U16 = mybir.dt.uint16
+U8 = mybir.dt.uint8
+FP8X4 = mybir.dt.float8_e4m3fn_x4
+FP4X4 = mybir.dt.float4_e2m1fn_x4
+ACT = mybir.ActivationFunctionType
+ALU = mybir.AluOpType
+
+P = 128
+PACK = 4
+NT = N // P
+HALF = 512
+WINDOW = 1368
+DIRECT = 256
+
+
+def tile_list_codes_through_tables_kernel(tc, ba_words, ba_scales, wa_words, wa_scales, bb, wb_words, wb_scales,
+                                               bc_words, bc_scales, wc_words, wc_scales, sc1, offs, offs2, offs3, out):
+    nc = tc.nc
+    with ExitStack() as ctx:
+        keep = ctx.enter_context(tc.tile_pool(name="keep", bufs=1))
+        ring = ctx.enter_context(tc.tile_pool(name="ring", bufs=1))
+        work = ctx.enter_context(tc.tile_pool(name="work", bufs=3))
+        psum = ctx.enter_context(tc.psum_pool(name="psum", bufs=1))
+
+        def plane(name):
+            return keep.tile([P, T], U8, name=name, align_bytes=64)
+
+        def load_plane(queue, t, scales, quadrants=range(4)):
+            for q in quadrants:
+                queue.dma_start(out=t[32 * q : 32 * q + 4, :].bitcast(I32), in_=scales[0, 4 * q : 4 * q + 4, :].bitcast(I32))
+
+        def load_fp4(name, words, queue=nc.sync):
+            t = keep.tile([P, 2 * T], U8, name=name, align_bytes=64)
+            queue.dma_start(out=t[:].bitcast(I32), in_=words[0].bitcast(I32))
+            return t
+
+        def load_fp8(name, words):
+            t = keep.tile([P, N], U32, name=name, align_bytes=64)
+            nc.sync.dma_start(out=t[:].bitcast(I32), in_=words[0].rearrange("p n r -> p (n r)").bitcast(I32))
+            return t
+
+        def load_list(name, src):
+            t = keep.tile([P, J // 16], U16, name=name)
+            nc.sync.dma_start(t[:], src)
+            return t
+
+        wa_s, ba_s = plane("wa_s"), plane("ba_s")
+        wc_s, bc_s, wb_s = plane("wc_s"), plane("bc_s"), plane("wb_s")
+        load_plane(nc.sync, ba_s, ba_scales, (0, 1))
+        load_plane(nc.scalar, wa_s, wa_scales, (0, 1))
+        wa_w = load_fp8("wa_w", wa_words)
+        ba_w = load_fp4("ba_w", ba_words, nc.scalar)
+        load_plane(nc.sync, ba_s, ba_scales, (2, 3))
+        load_plane(nc.scalar, wa_s, wa_scales, (2, 3))
+        list_a = load_list("list_a", offs)
+        raw = ring.tile([P, PACK, T], F32, name="raw", tag="g3", align_bytes=64)
+        nc.sync.dma_start(out=raw[:], in_=bb.rearrange("(p r) t -> p r t", r=PACK))
+        bc_w = load_fp4("bc_w", bc_words)
+        wc_w = load_fp8("wc_w", wc_words)
+        load_plane(nc.sync, wc_s, wc_scales)
+        load_plane(nc.sync, bc_s, bc_scales)
+        list_c = load_list("list_c", offs3)
+        wb_w = load_fp4("wb_w", wb_words)
+        load_plane(nc.sync, wb_s, wb_scales)
+        list_b = load_list("list_b", offs2)
+        scale = keep.tile([P, J // P], F32, name="scale")
+        with nc.allow_non_contiguous_dma(reason="one scale a partition"):
+            nc.sync.dma_start(out=scale[:], in_=sc1[0].rearrange("(b p) -> p b", p=P))
+        scale_row = keep.tile([P, DIRECT], F32, name="scale_row")
+        nc.sync.dma_start(out=scale_row[:], in_=sc1[0, J - DIRECT :].partition_broadcast(P))
+
+        ident = keep.tile([P, P], F32, name="ident")
+        make_identity(nc, ident[:])
+
+        tables = {(name, i): keep.tile([P, WINDOW], F32, name="z%s%d" % (name, i)) for name in "acb" for i in range(NT)}
+        lists = {"a": list_a, "c": list_c, "b": list_b}
+
+        def product(name, i, bank, lhsT, lhsT_scale, rhs, rhs_scale):
+            acc = psum.tile([P, T], F32, name="acc", tag=bank)
+            nc.tensor.matmul_mx(out=acc[:], lhsT=lhsT, lhsT_scale=lhsT_scale, rhs=rhs, rhs_scale=rhs_scale, start=True, stop=True)
+            nc.scalar.copy(out=tables[name, i][:, :T], in_=acc[:])
+
+        for h, (bank, copy) in enumerate((("z0", nc.scalar.copy), ("s0", nc.vector.tensor_copy))):
+            cols = slice(h * T // 2, (h + 1) * T // 2)
+            acc = psum.tile([P, T // 2], F32, name="acc", tag=bank)
+            nc.tensor.matmul_mx(out=acc[:], lhsT=wa_w[:, :P].bitcast(FP8X4), lhsT_scale=wa_s[:, :P],
+                                rhs=ba_w[:, h * T : (h + 1) * T].bitcast(FP4X4), rhs_scale=ba_s[:, cols], start=True, stop=True)
+            copy(out=tables["a", 0][:, cols], in_=acc[:])
+        for i, bank in ((1, "z1"), (2, "k0"), (3, "k1")):
+            cols = slice(i * P, (i + 1) * P)
+            product("a", i, bank, wa_w[:, cols].bitcast(FP8X4), wa_s[:, cols], ba_w[:].bitcast(FP4X4), ba_s[:])
+
+        grouped = ring.tile([P, T, PACK], BF16, name="grouped", tag="g2", align_bytes=64)
+        nc.scalar.copy(out=grouped[:], in_=raw[:].rearrange("p r t -> p t r"))
+        bb_w = keep.tile([P, T], U32, name="bb_w", align_bytes=64)
+        bb_s = keep.tile([P, T], U8, name="bb_s", align_bytes=64)
+        nc.vector.quantize_mx(out=bb_w[:].bitcast(FP8X4), scales=bb_s[:], in_=grouped[:].rearrange("p t r -> p (t r)"))
+
+        for i, bank in enumerate(("s2", "s3", "z0", "z1")):
+            cols = slice(i * P, (i + 1) * P)
+            product("c", i, bank, wc_w[:, cols].bitcast(FP8X4), wc_s[:, cols], bc_w[:].bitcast(FP4X4), bc_s[:])
+        for i, bank in enumerate(("k0", "k1", "z0", "z1")):
+            cols = slice(i * P, (i + 1) * P)
+            product("b", i, bank, wb_w[:, 2 * i * P : 2 * (i + 1) * P].bitcast(FP4X4), wb_s[:, cols], bb_w[:].bitcast(FP8X4), bb_s[:])
+
+        sum_banks = (("s0", "s1"), ("s2", "s3"), ("z0", "z1"), ("s0", "s1"))
+        sums = {}
+
+        def finish(i, h, blocks):
+            total = sums[i, h]
+            width = blocks * P
+            relu = work.tile([P, blocks, P], F32, name="relu")
+            nc.scalar.activation(out=relu[:], in_=total[:], func=ACT.Relu)
+            scaled = work.tile([P, blocks, P], F32, name="scaled")
+            for q in range(blocks):
+                nc.scalar.activation(out=scaled[:, q, :], in_=relu[:, q, :], func=ACT.Copy, scale=scale[:, 4 * h + q : 4 * h + q + 1])
+            back = psum.tile([P, blocks, P], F32, name="back", tag="k%d" % h)
+            for q in range(blocks):
+                nc.tensor.transpose(back[:, q, :], scaled[:, q, :], ident[:])
+            result = work.tile([P, width], F32, name="result")
+            nc.scalar.copy(out=result[:], in_=back[:].rearrange("p q j -> p (q j)"))
+            nc.sync.dma_start(out=out[i * P : (i + 1) * P, h * HALF : h * HALF + width], in_=result[:])
+
+        def look_up(name, i, j0, j1):
+            return tables[name, i][:].indirect(lists[name][:, j0 // 16 : j1 // 16])
+
+        order = [("a", 0), ("a", 1), ("c", 0), ("c", 1), ("b", 0), ("b", 1)] + [(name, i) for i in (2, 3) for name in "acb"]
+        for step, (name, i) in enumerate(order):
+            width = J - DIRECT if i == NT - 1 else J
+            picked = ring.tile([P, width], F32, name="picked", tag="g%d" % (step % 4), align_bytes=64)
+            last = step == len(order) - 1
+            if not last:
+                nc.vector.tensor_copy(out=picked[:], in_=look_up(name, i, 0, width))
+            for h in range(2):
+                blocks = min(HALF, width - h * HALF) // P
+                if last:
+                    nc.vector.tensor_copy(out=picked[:, h * HALF : h * HALF + blocks * P], in_=look_up(name, i, h * HALF, h * HALF + blocks * P))
+                if name == "a":
+                    sums[i, h] = psum.tile([P, blocks, P], F32, name="total", tag=sum_banks[i][h])
+                for q in range(blocks):
+                    j0 = h * HALF + q * P
+                    nc.tensor.matmul(sums[i, h][:, q, :], lhsT=picked[:, j0 : j0 + P], rhs=ident[:], is_transpose=True,
+                                     start=(name == "a" and q == 0), stop=(name == "b" and q == blocks - 1))
+                if name == "b":
+                    finish(i, h, blocks)
+
+        i = NT - 1
+        part_a = ring.tile([P, DIRECT], F32, name="part_a", tag="g2", align_bytes=64)
+        nc.vector.tensor_copy(out=part_a[:], in_=look_up("a", i, J - DIRECT, J))
+        part_ac = work.tile([P, DIRECT], F32, name="part_ac")
+        nc.vector.tensor_tensor(out=part_ac[:], in0=look_up("c", i, J - DIRECT, J), in1=part_a[:], op=ALU.add)
+        part_acb = work.tile([P, DIRECT], F32, name="part_acb")
+        nc.vector.tensor_tensor(out=part_acb[:], in0=look_up("b", i, J - DIRECT, J), in1=part_ac[:], op=ALU.add)
+        part_out = work.tile([P, DIRECT], F32, name="part_out")
+        nc.vector.scalar_tensor_tensor(out=part_out[:], in0=part_acb[:], scalar=0.0, in1=scale_row[:], op0=ALU.max, op1=ALU.mult)
+        nc.sync.dma_start(out=out[i * P : (i + 1) * P, J - DIRECT :], in_=part_out[:])

@@ -31,7 +31,7 @@ def tile_list_codes_through_tables_kernel(tc, ba_words, ba_scales, wa_words, wa_
     with ExitStack() as ctx:
         keep = ctx.enter_context(tc.tile_pool(name="keep", bufs=1))
         ring = ctx.enter_context(tc.tile_pool(name="ring", bufs=1))
-        work = ctx.enter_context(tc.tile_pool(name="work", bufs=3))
+        work = ctx.enter_context(tc.tile_pool(name="work", bufs=4))
         psum = ctx.enter_context(tc.psum_pool(name="psum", bufs=1))
 
         def plane(name):
@@ -84,7 +84,7 @@ def tile_list_codes_through_tables_kernel(tc, ba_words, ba_scales, wa_words, wa_
         ident = keep.tile([P, P], F32, name="ident")
         make_identity(nc, ident[:])
 
-        tables = {(name, i): keep.tile([P, WINDOW], F32, name="z%s%d" % (name, i)) for name in "acb" for i in range(NT)}
+        tables = {(name, i): keep.tile([P, J if i == NT - 1 else WINDOW], F32, name="z%s%d" % (name, i)) for name in "acb" for i in range(NT)}
         lists = {"a": list_a, "c": list_c, "b": list_b}
 
         def product(name, i, bank, lhsT, lhsT_scale, rhs, rhs_scale):
@@ -118,14 +118,17 @@ def tile_list_codes_through_tables_kernel(tc, ba_words, ba_scales, wa_words, wa_
         sum_banks = (("s0", "s1"), ("s2", "s3"), ("z0", "z1"), ("s0", "s1"))
         sums = {}
 
-        def finish(i, h, blocks):
+        def activate(i, h, blocks):
             total = sums[i, h]
-            width = blocks * P
             relu = work.tile([P, blocks, P], F32, name="relu")
             nc.scalar.activation(out=relu[:], in_=total[:], func=ACT.Relu)
             scaled = work.tile([P, blocks, P], F32, name="scaled")
             for q in range(blocks):
                 nc.scalar.activation(out=scaled[:, q, :], in_=relu[:, q, :], func=ACT.Copy, scale=scale[:, 4 * h + q : 4 * h + q + 1])
+            return scaled
+
+        def finish(i, h, blocks, scaled):
+            width = blocks * P
             back = psum.tile([P, blocks, P], F32, name="back", tag="k%d" % h)
             for q in range(blocks):
                 nc.tensor.transpose(back[:, q, :], scaled[:, q, :], ident[:])
@@ -136,33 +139,42 @@ def tile_list_codes_through_tables_kernel(tc, ba_words, ba_scales, wa_words, wa_
         def look_up(name, i, j0, j1):
             return tables[name, i][:].indirect(lists[name][:, j0 // 16 : j1 // 16])
 
-        order = [("a", 0), ("a", 1), ("c", 0), ("c", 1), ("b", 0), ("b", 1)] + [(name, i) for i in (2, 3) for name in "acb"]
-        for step, (name, i) in enumerate(order):
-            width = J - DIRECT if i == NT - 1 else J
-            picked = ring.tile([P, width], F32, name="picked", tag="g%d" % (step % 4), align_bytes=64)
-            last = step == len(order) - 1
-            if not last:
-                nc.vector.tensor_copy(out=picked[:], in_=look_up(name, i, 0, width))
-            for h in range(2):
-                blocks = min(HALF, width - h * HALF) // P
-                if last:
-                    nc.vector.tensor_copy(out=picked[:, h * HALF : h * HALF + blocks * P], in_=look_up(name, i, h * HALF, h * HALF + blocks * P))
+        last = NT - 1
+        order = [(name, i, 0, J) for name in "acb" for i in (0, 1)] + [(name, 2, 0, J) for name in "acb"]
+        order = order + [("a", last, 0, J - DIRECT)] + [(name, last, j0, j1) for j0, j1 in ((0, HALF), (HALF, J - DIRECT)) for name in "cb"]
+        pending = []
+        for step, (name, i, j0, j1) in enumerate(order):
+            ready, pending = (pending, []) if name != "c" else ([], pending)
+            picked = ring.tile([P, j1 - j0], F32, name="picked", tag="g%d" % (step % 4), align_bytes=64)
+            nc.vector.tensor_copy(out=picked[:], in_=look_up(name, i, j0, j1))
+            for start in range(j0, j1, HALF):
+                h = start // HALF
+                blocks = min(HALF, j1 - start) // P
                 if name == "a":
                     sums[i, h] = psum.tile([P, blocks, P], F32, name="total", tag=sum_banks[i][h])
                 for q in range(blocks):
-                    j0 = h * HALF + q * P
-                    nc.tensor.matmul(sums[i, h][:, q, :], lhsT=picked[:, j0 : j0 + P], rhs=ident[:], is_transpose=True,
+                    col = start - j0 + q * P
+                    nc.tensor.matmul(sums[i, h][:, q, :], lhsT=picked[:, col : col + P], rhs=ident[:], is_transpose=True,
                                      start=(name == "a" and q == 0), stop=(name == "b" and q == blocks - 1))
                 if name == "b":
-                    finish(i, h, blocks)
+                    pending.append((i, h, blocks, activate(i, h, blocks)))
+            for args in ready:
+                finish(*args)
+        for args in pending:
+            finish(*args)
 
-        i = NT - 1
-        part_a = ring.tile([P, DIRECT], F32, name="part_a", tag="g2", align_bytes=64)
-        nc.vector.tensor_copy(out=part_a[:], in_=look_up("a", i, J - DIRECT, J))
+        chains = [slice(c0, c0 + P) for c0 in range(0, DIRECT, P)]
+        part_a = ring.tile([P, DIRECT], F32, name="part_a", tag="g%d" % (len(order) % 4), align_bytes=64)
         part_ac = work.tile([P, DIRECT], F32, name="part_ac")
-        nc.vector.tensor_tensor(out=part_ac[:], in0=look_up("c", i, J - DIRECT, J), in1=part_a[:], op=ALU.add)
         part_acb = work.tile([P, DIRECT], F32, name="part_acb")
-        nc.vector.tensor_tensor(out=part_acb[:], in0=look_up("b", i, J - DIRECT, J), in1=part_ac[:], op=ALU.add)
         part_out = work.tile([P, DIRECT], F32, name="part_out")
-        nc.vector.scalar_tensor_tensor(out=part_out[:], in0=part_acb[:], scalar=0.0, in1=scale_row[:], op0=ALU.max, op1=ALU.mult)
-        nc.sync.dma_start(out=out[i * P : (i + 1) * P, J - DIRECT :], in_=part_out[:])
+        base = J - DIRECT
+        for c in chains:
+            nc.vector.tensor_copy(out=part_a[:, c], in_=look_up("a", last, base + c.start, base + c.stop))
+        for c in chains:
+            nc.vector.tensor_tensor(out=part_ac[:, c], in0=look_up("c", last, base + c.start, base + c.stop), in1=part_a[:, c], op=ALU.add)
+        for c in chains:
+            nc.vector.tensor_tensor(out=part_acb[:, c], in0=look_up("b", last, base + c.start, base + c.stop), in1=part_ac[:, c], op=ALU.add)
+        for c in chains:
+            nc.vector.scalar_tensor_tensor(out=part_out[:, c], in0=part_acb[:, c], scalar=0.0, in1=scale_row[:, c], op0=ALU.max, op1=ALU.mult)
+        nc.sync.dma_start(out=out[last * P :, base:], in_=part_out[:])

from contextlib import ExitStack

import concourse.mybir as mybir
from concourse.masks import make_identity

K, T, J, N = 512, 512, 1024, 512
FLOPS = 3 * 2 * K * T * N

F32 = mybir.dt.float32
BF16 = mybir.dt.bfloat16
I32 = mybir.dt.int32
U32 = mybir.dt.uint32
U16 = mybir.dt.uint16
U8 = mybir.dt.uint8
FP8X4 = mybir.dt.float8_e4m3fn_x4
FP4X4 = mybir.dt.float4_e2m1fn_x4
ACT = mybir.ActivationFunctionType
ALU = mybir.AluOpType

P = 128
PACK = 4
NT = N // P
HALF = 512
WINDOW = 1368
DIRECT = 256


def tile_list_codes_through_tables_kernel(tc, ba_words, ba_scales, wa_words, wa_scales, bb, wb_words, wb_scales,
                                               bc_words, bc_scales, wc_words, wc_scales, sc1, offs, offs2, offs3, out):
    nc = tc.nc
    with ExitStack() as ctx:
        keep = ctx.enter_context(tc.tile_pool(name="keep", bufs=1))
        ring = ctx.enter_context(tc.tile_pool(name="ring", bufs=1))
        work = ctx.enter_context(tc.tile_pool(name="work", bufs=4))
        psum = ctx.enter_context(tc.psum_pool(name="psum", bufs=1))

        def plane(name):
            return keep.tile([P, T], U8, name=name, align_bytes=64)

        def load_plane(queue, t, scales, quadrants=range(4)):
            for q in quadrants:
                queue.dma_start(out=t[32 * q : 32 * q + 4, :].bitcast(I32), in_=scales[0, 4 * q : 4 * q + 4, :].bitcast(I32))

        def load_fp4(name, words, queue=nc.sync):
            t = keep.tile([P, 2 * T], U8, name=name, align_bytes=64)
            queue.dma_start(out=t[:].bitcast(I32), in_=words[0].bitcast(I32))
            return t

        def load_fp8(name, words):
            t = keep.tile([P, N], U32, name=name, align_bytes=64)
            nc.sync.dma_start(out=t[:].bitcast(I32), in_=words[0].rearrange("p n r -> p (n r)").bitcast(I32))
            return t

        def load_list(name, src):
            t = keep.tile([P, J // 16], U16, name=name)
            nc.sync.dma_start(t[:], src)
            return t

        wa_s, ba_s = plane("wa_s"), plane("ba_s")
        wc_s, bc_s, wb_s = plane("wc_s"), plane("bc_s"), plane("wb_s")
        load_plane(nc.sync, ba_s, ba_scales, (0, 1))
        load_plane(nc.scalar, wa_s, wa_scales, (0, 1))
        wa_w = load_fp8("wa_w", wa_words)
        ba_w = load_fp4("ba_w", ba_words, nc.scalar)
        load_plane(nc.sync, ba_s, ba_scales, (2, 3))
        load_plane(nc.scalar, wa_s, wa_scales, (2, 3))
        list_a = load_list("list_a", offs)
        raw = ring.tile([P, PACK, T], F32, name="raw", tag="g3", align_bytes=64)
        nc.sync.dma_start(out=raw[:], in_=bb.rearrange("(p r) t -> p r t", r=PACK))
        bc_w = load_fp4("bc_w", bc_words)
        wc_w = load_fp8("wc_w", wc_words)
        load_plane(nc.sync, wc_s, wc_scales)
        load_plane(nc.sync, bc_s, bc_scales)
        list_c = load_list("list_c", offs3)
        wb_w = load_fp4("wb_w", wb_words)
        load_plane(nc.sync, wb_s, wb_scales)
        list_b = load_list("list_b", offs2)
        scale = keep.tile([P, J // P], F32, name="scale")
        with nc.allow_non_contiguous_dma(reason="one scale a partition"):
            nc.sync.dma_start(out=scale[:], in_=sc1[0].rearrange("(b p) -> p b", p=P))
        scale_row = keep.tile([P, DIRECT], F32, name="scale_row")
        nc.sync.dma_start(out=scale_row[:], in_=sc1[0, J - DIRECT :].partition_broadcast(P))

        ident = keep.tile([P, P], F32, name="ident")
        make_identity(nc, ident[:])

        tables = {(name, i): keep.tile([P, J if i == NT - 1 else WINDOW], F32, name="z%s%d" % (name, i)) for name in "acb" for i in range(NT)}
        lists = {"a": list_a, "c": list_c, "b": list_b}

        def product(name, i, bank, lhsT, lhsT_scale, rhs, rhs_scale):
            acc = psum.tile([P, T], F32, name="acc", tag=bank)
            nc.tensor.matmul_mx(out=acc[:], lhsT=lhsT, lhsT_scale=lhsT_scale, rhs=rhs, rhs_scale=rhs_scale, start=True, stop=True)
            nc.scalar.copy(out=tables[name, i][:, :T], in_=acc[:])

        for h, (bank, copy) in enumerate((("z0", nc.scalar.copy), ("s0", nc.vector.tensor_copy))):
            cols = slice(h * T // 2, (h + 1) * T // 2)
            acc = psum.tile([P, T // 2], F32, name="acc", tag=bank)
            nc.tensor.matmul_mx(out=acc[:], lhsT=wa_w[:, :P].bitcast(FP8X4), lhsT_scale=wa_s[:, :P],
                                rhs=ba_w[:, h * T : (h + 1) * T].bitcast(FP4X4), rhs_scale=ba_s[:, cols], start=True, stop=True)
            copy(out=tables["a", 0][:, cols], in_=acc[:])
        for i, bank in ((1, "z1"), (2, "k0"), (3, "k1")):
            cols = slice(i * P, (i + 1) * P)
            product("a", i, bank, wa_w[:, cols].bitcast(FP8X4), wa_s[:, cols], ba_w[:].bitcast(FP4X4), ba_s[:])

        grouped = ring.tile([P, T, PACK], BF16, name="grouped", tag="g2", align_bytes=64)
        nc.scalar.copy(out=grouped[:], in_=raw[:].rearrange("p r t -> p t r"))
        bb_w = keep.tile([P, T], U32, name="bb_w", align_bytes=64)
        bb_s = keep.tile([P, T], U8, name="bb_s", align_bytes=64)
        nc.vector.quantize_mx(out=bb_w[:].bitcast(FP8X4), scales=bb_s[:], in_=grouped[:].rearrange("p t r -> p (t r)"))

        for i, bank in enumerate(("s2", "s3", "z0", "z1")):
            cols = slice(i * P, (i + 1) * P)
            product("c", i, bank, wc_w[:, cols].bitcast(FP8X4), wc_s[:, cols], bc_w[:].bitcast(FP4X4), bc_s[:])
        for i, bank in enumerate(("k0", "k1", "z0", "z1")):
            cols = slice(i * P, (i + 1) * P)
            product("b", i, bank, wb_w[:, 2 * i * P : 2 * (i + 1) * P].bitcast(FP4X4), wb_s[:, cols], bb_w[:].bitcast(FP8X4), bb_s[:])

        sum_banks = (("s0", "s1"), ("s2", "s3"), ("z0", "z1"), ("s0", "s1"))
        sums = {}

        def activate(i, h, blocks):
            total = sums[i, h]
            relu = work.tile([P, blocks, P], F32, name="relu")
            nc.scalar.activation(out=relu[:], in_=total[:], func=ACT.Relu)
            scaled = work.tile([P, blocks, P], F32, name="scaled")
            for q in range(blocks):
                nc.scalar.activation(out=scaled[:, q, :], in_=relu[:, q, :], func=ACT.Copy, scale=scale[:, 4 * h + q : 4 * h + q + 1])
            return scaled

        def finish(i, h, blocks, scaled):
            width = blocks * P
            back = psum.tile([P, blocks, P], F32, name="back", tag="k%d" % h)
            for q in range(blocks):
                nc.tensor.transpose(back[:, q, :], scaled[:, q, :], ident[:])
            result = work.tile([P, width], F32, name="result")
            nc.scalar.copy(out=result[:], in_=back[:].rearrange("p q j -> p (q j)"))
            nc.sync.dma_start(out=out[i * P : (i + 1) * P, h * HALF : h * HALF + width], in_=result[:])

        def look_up(name, i, j0, j1):
            return tables[name, i][:].indirect(lists[name][:, j0 // 16 : j1 // 16])

        last = NT - 1
        order = [(name, i, 0, J) for name in "acb" for i in (0, 1)] + [(name, 2, 0, J) for name in "acb"]
        order = order + [("a", last, 0, J - DIRECT)] + [(name, last, j0, j1) for j0, j1 in ((0, HALF), (HALF, J - DIRECT)) for name in "cb"]
        pending = []
        for step, (name, i, j0, j1) in enumerate(order):
            ready, pending = (pending, []) if name != "c" else ([], pending)
            picked = ring.tile([P, j1 - j0], F32, name="picked", tag="g%d" % (step % 4), align_bytes=64)
            nc.vector.tensor_copy(out=picked[:], in_=look_up(name, i, j0, j1))
            for start in range(j0, j1, HALF):
                h = start // HALF
                blocks = min(HALF, j1 - start) // P
                if name == "a":
                    sums[i, h] = psum.tile([P, blocks, P], F32, name="total", tag=sum_banks[i][h])
                for q in range(blocks):
                    col = start - j0 + q * P
                    nc.tensor.matmul(sums[i, h][:, q, :], lhsT=picked[:, col : col + P], rhs=ident[:], is_transpose=True,
                                     start=(name == "a" and q == 0), stop=(name == "b" and q == blocks - 1))
                if name == "b":
                    pending.append((i, h, blocks, activate(i, h, blocks)))
            for args in ready:
                finish(*args)
        for args in pending:
            finish(*args)

        chains = [slice(c0, c0 + P) for c0 in range(0, DIRECT, P)]
        part_a = ring.tile([P, DIRECT], F32, name="part_a", tag="g%d" % (len(order) % 4), align_bytes=64)
        part_ac = work.tile([P, DIRECT], F32, name="part_ac")
        part_acb = work.tile([P, DIRECT], F32, name="part_acb")
        part_out = work.tile([P, DIRECT], F32, name="part_out")
        base = J - DIRECT
        for c in chains:
            nc.vector.tensor_copy(out=part_a[:, c], in_=look_up("a", last, base + c.start, base + c.stop))
        for c in chains:
            nc.vector.tensor_tensor(out=part_ac[:, c], in0=look_up("c", last, base + c.start, base + c.stop), in1=part_a[:, c], op=ALU.add)
        for c in chains:
            nc.vector.tensor_tensor(out=part_acb[:, c], in0=look_up("b", last, base + c.start, base + c.stop), in1=part_ac[:, c], op=ALU.add)
        for c in chains:
            nc.vector.scalar_tensor_tensor(out=part_out[:, c], in0=part_acb[:, c], scalar=0.0, in1=scale_row[:, c], op0=ALU.max, op1=ALU.mult)
        nc.sync.dma_start(out=out[last * P :, base:], in_=part_out[:])
